import numpy as np
import ml_dtypes


def mxq(x, axis, fmt="e4m3"):
    dtype, down = {"e4m3": (ml_dtypes.float8_e4m3fn, 7), "e5m2": (ml_dtypes.float8_e5m2, 14)}[fmt]
    v = np.moveaxis(np.asarray(x, np.float32).astype(ml_dtypes.bfloat16).astype(np.float64), axis, -1)
    blocks = v.reshape(v.shape[:-1] + (-1, 32))
    amax = np.abs(blocks).max(-1, keepdims=True)
    byte = np.maximum(np.where(amax > 0, np.frexp(amax)[1] - 1 + 127, 0) - down, 1)
    scale = np.exp2(byte - 127.0)
    codes = (blocks / scale).astype(np.float32).astype(dtype).astype(np.float64)
    return np.moveaxis((codes * scale).reshape(v.shape), -1, axis)


WIDE = False


def mx_kscale(k):
    if not WIDE:
        return np.ones(k)
    levels = np.array([10, -10, 5, -5, 0])
    if k % 512:
        return np.exp2(np.random.permutation(np.resize(levels, k // 32))).repeat(32)
    a = np.empty((k // 512, 16))
    for p in range(k // 512):
        a[p, :8] = np.random.permutation(np.resize(levels, 8))
        for g in range(8):
            far = levels[np.abs(levels - a[p, g]) >= 10]
            a[p, g + 8] = far[np.random.randint(len(far))]
    return np.exp2(a.ravel()).repeat(32)


def f64(x):
    return np.asarray(x).astype(np.float64)


def striped(idx):
    return np.tile(idx.reshape(-1, 16).T, (8, 1)).astype(np.uint16)


def unstriped(offs):
    return offs[:16].T.reshape(-1).astype(np.int64)


E2M1 = np.array([0.0, 0.5, 1.0, 1.5, 2.0, 3.0, 4.0, 6.0, -0.0, -0.5, -1.0, -1.5, -2.0, -3.0, -4.0, -6.0])


def pack_weight(w, fmt):
    k, n = w.shape
    w = f64(np.asarray(w, np.float32).astype(ml_dtypes.bfloat16)).reshape(k // 32, 32, n)
    amax = np.abs(w).max(1)
    if fmt == "e4m3":
        byte = np.frexp(amax)[1] - 1 + 127 - 7
    else:
        mant, ex = np.frexp(amax / 6.0)
        byte = np.where(mant > 0.5, ex, ex - 1) + 127
    byte = np.clip(np.where(amax > 0, byte, 1), 1, 254)
    scaled = (w * np.exp2(127.0 - byte)[:, None, :]).reshape(k, n).astype(np.float32)
    by_word = np.ascontiguousarray(scaled.reshape(k // 512, 128, 4, n).transpose(0, 1, 3, 2))
    if fmt == "e4m3":
        words = by_word.astype(ml_dtypes.float8_e4m3fn).view(np.uint8)
    else:
        c = by_word.astype(ml_dtypes.float4_e2m1fn).view(np.uint8) & 0xF
        words = (c[..., 0::2] | (c[..., 1::2] << 4)).reshape(k // 512, 128, 2 * n)
    return np.ascontiguousarray(words), np.ascontiguousarray(byte.astype(np.uint8).reshape(k // 512, 16, n))


def unpack_weight(words, scales, fmt):
    g, _, n = scales.shape
    words = np.ascontiguousarray(words).reshape(g, 128, n, -1)
    if fmt == "e4m3":
        vals = words.view(ml_dtypes.float8_e4m3fn).astype(np.float64)
    else:
        nib = np.empty((g, 128, n, 4), np.uint8)
        nib[..., 0::2] = words & 0xF
        nib[..., 1::2] = words >> 4
        vals = E2M1[nib]
    vals = vals * np.repeat(np.exp2(scales.astype(np.float64) - 127.0), 8, axis=1)[..., None]
    return vals.transpose(0, 1, 3, 2).reshape(g * 512, n)


def planes(y):
    n, m = y.shape
    v = y.astype(np.float32).astype(ml_dtypes.bfloat16).astype(np.float64).reshape(n // 32, 32, m)
    top = np.abs(v).max(1)
    byte = np.clip(np.where(top > 0, np.frexp(top)[1] - 1 + 127 - 7, 1), 1, 254)
    codes = (v * np.exp2(127.0 - byte)[:, None, :]).reshape(n, m).astype(np.float32).astype(ml_dtypes.float8_e4m3fn).view(np.uint8)
    words = codes.reshape(n // 512, 128, 4, m).transpose(0, 1, 3, 2)
    return np.ascontiguousarray(words), np.ascontiguousarray(byte.astype(np.uint8).reshape(n // 512, 16, m))


def gelu(v):
    return 0.5 * v * (1.0 + np.tanh(np.sqrt(2.0 / np.pi) * (v + 0.044715 * v**3)))


K, T, E, C, H, N = 1024, 640, 10, 128, 512, 512


def by_expert(wq, xq):
    return np.concatenate([wq[e].T @ xq[:, e * C:(e + 1) * C] for e in range(E)], axis=1)


def setup_inputs():
    n = np.random.standard_normal
    s = mx_kscale(K)
    u = mx_kscale(H)
    first = np.random.permutation(np.repeat(np.arange(E), T // E))
    second = (first + 1 + np.random.permutation(np.repeat(np.arange(E - 1), -(-T // (E - 1)))[:T])) % E
    while np.bincount(second, minlength=E).max() != T // E:
        load = np.bincount(second, minlength=E); hi, lo = int(load.argmax()), int(load.argmin())
        t = np.flatnonzero((second == hi) & (first != lo))[0]; second[t] = lo
    slot_token = np.empty(E * C, np.int64); pos = np.empty((2, T), np.int64); fill = np.zeros(E, np.int64)
    place = np.stack([np.random.permutation(C) for _ in range(E)])
    for r, deal in enumerate((first, second)):
        for t in np.random.permutation(T):
            e = deal[t]; j = e * C + place[e, fill[e]]; fill[e] += 1; slot_token[j] = t; pos[r, t] = j
    g = np.random.uniform(0.2, 0.8, T)
    x = pack_weight(n((K, T)) * s[:, None], "e4m3")
    w2 = pack_weight(n((H, N)) / np.sqrt(H) / u[:, None], "e4m3")
    return {
        "x_words": x[0],
        "x_scales": x[1],
        "w1": (n((E, K, H)) / np.sqrt(K) / s[None, :, None] * u).astype(np.float32),
        "w2_words": w2[0],
        "w2_scales": w2[1],
        "gate": np.stack([np.tile(g, (128, 1)), np.tile(1.0 - g, (128, 1))]).astype(np.float32),
        "offs": striped(slot_token),
        "pos1": striped(pos[0]),
        "pos2": striped(pos[1]),
    }


def reference(x_words, x_scales, w1, w2_words, w2_scales, gate, offs, pos1, pos2):
    w1q = mxq(f64(w1), 1, "e4m3")
    w2 = unpack_weight(w2_words, w2_scales, "e4m3")
    idx = unstriped(offs)
    xq = unpack_weight(x_words, x_scales, "e4m3")[:, idx]
    h = gelu(by_expert(w1q, xq))
    c = sum(f64(gate[r, :1]) * h[:, unstriped(p)] for r, p in enumerate((pos1, pos2)))
    out_0 = w2.T @ mxq(c, 0, "e4m3")
    return (out_0,) + planes(out_0)

@@ -1,0 +1,308 @@
+from contextlib import ExitStack
+
+import concourse.mybir as mybir
+from concourse.masks import make_identity
+
+K, T, E, C, H, N = 1024, 640, 10, 128, 512, 512
+FLOPS = 2 * E * C * K * H + 2 * T * H * N
+
+F32 = mybir.dt.float32
+BF16 = mybir.dt.bfloat16
+I32 = mybir.dt.int32
+U32 = mybir.dt.uint32
+U16 = mybir.dt.uint16
+U8 = mybir.dt.uint8
+FP8X4 = mybir.dt.float8_e4m3fn_x4
+MULT = mybir.AluOpType.mult
+GELU = mybir.ActivationFunctionType.Gelu_apprx_tanh
+
+P = 128
+PASSES = K // 512
+QUARTERS = H // P
+SLOTS = E * C
+TOKEN_TILES = T // P
+GATHER_SLOTS = 256
+GROUPS = ((0, 2), (2, 4), (4, 5))
+
+
+def tile_moe_sdn_lin_gelu_kernel(
+    tc, x_words, x_scales, w1, w2_words, w2_scales, gate, offs, pos1, pos2, out_0, out_1, out_2
+):
+    nc = tc.nc
+    with ExitStack() as ctx:
+        lists = ctx.enter_context(tc.tile_pool(name="lists", bufs=1))
+        keep = ctx.enter_context(tc.tile_pool(name="keep", bufs=1))
+        stage = ctx.enter_context(tc.tile_pool(name="stage", bufs=2))
+        psum = ctx.enter_context(tc.psum_pool(name="psum", bufs=1))
+
+        offs_sb = lists.tile([P, SLOTS // 16], U16, name="offs_sb")
+        pos_sb = [lists.tile([P, T // 16], U16, name="pos%d_sb" % r) for r in range(2)]
+        xw = keep.tile([P, PASSES, T], I32, name="xw", align_bytes=64)
+        xs = keep.tile([P, T], U8, name="xs", align_bytes=64)
+        ident = keep.tile([P, P], F32, name="ident")
+        gate_rows = keep.tile([P, P], F32, name="gate_rows")
+        gate_cols = keep.tile([P, 16], F32, name="gate_cols")
+        gate_sb = [keep.tile([P, T], F32, name="gate%d_sb" % r) for r in range(2)]
+        w2_raw = keep.tile([P, N], I32, name="w2_raw")
+        s2_raw = keep.tile([P, N], U8, name="s2_raw")
+        w2_codes = keep.tile([P, N], I32, name="w2_codes", align_bytes=64)
+        w2_planes = keep.tile([P, N], U8, name="w2_planes", align_bytes=64)
+        h = [keep.tile([P, SLOTS], F32, name="h%d" % q) for q in range(QUARTERS)]
+        xg = {}
+        xsg = {}
+        c_rows = [keep.tile([P, b - a, H], BF16, name="c_rows%d" % a) for a, b in GROUPS]
+        out_scales = keep.tile([P, T], U8, name="out_scales", align_bytes=64)
+
+        nc.vector.memset(xs[:].bitcast(I32), 0)
+        nc.vector.memset(s2_raw[:].bitcast(I32), 0)
+        nc.vector.memset(gate_rows[:], 0.0)
+        make_identity(nc, ident[:])
+
+        def load_group(e0, e1, c0, c1):
+            slabs = PASSES * (e1 - e0)
+            raw = stage.tile([P, slabs, 4, c1 - c0], F32, name="raw", bufs=5)
+            rows = w1[e0:e1, :, c0:c1].rearrange("e (s p j) c -> p (e s) j c", p=P, j=4)
+            if slabs > 4:
+                for j in range(4):
+                    nc.sync.dma_start(out=raw[:, :, j, :], in_=rows[:, :, j, :])
+            else:
+                for i in range(slabs):
+                    nc.sync.dma_start(out=raw[:, i, :, :], in_=rows[:, i, :, :])
+                    for extra in extras.pop((e0, c0, i), []):
+                        extra()
+            return raw
+
+        def cast(engine_copy, grouped, raw, a, b):
+            engine_copy(
+                out=grouped[:, 4 * a : 4 * b].rearrange("p (c i j) -> p c j i", i=4, j=4),
+                in_=raw[:, :, a:b].rearrange("p j (c i) -> p c j i", i=4),
+            )
+
+        def cast_columns(engine_copy, grouped, slabs, a, b):
+            width = slabs.shape[3]
+            while a < b:
+                i, c = divmod(a, width)
+                if c == 0 and b - a >= width:
+                    n = (b - a) // width
+                    engine_copy(
+                        out=grouped[:, 4 * a : 4 * (a + n * width)].rearrange("p (s c i j) -> p s c j i", s=n, i=4, j=4),
+                        in_=slabs[:, i : i + n, :, :].rearrange("p s j (c i) -> p s c j i", i=4),
+                    )
+                    a = a + n * width
+                else:
+                    end = min(b, (i + 1) * width)
+                    engine_copy(
+                        out=grouped[:, 4 * a : 4 * end].rearrange("p (c i j) -> p c j i", i=4, j=4),
+                        in_=slabs[:, i, :, c : end - i * width].rearrange("p j (c i) -> p c j i", i=4),
+                    )
+                    a = end
+
+        def expert_unit(slabs, e0, c0, scalar_eighths, tie, bank):
+            count, width = slabs.shape[1], slabs.shape[3]
+            experts = count // PASSES
+            columns = count * width
+            if tie is None:
+                grouped = stage.tile([P, 4 * columns], BF16, name="grouped", bufs=3, align_bytes=64)
+            else:
+                grouped = stage.tile([P, 4 * columns], BF16, name="tied_grouped", tag=tie, bufs=1, align_bytes=64)
+            split = columns * scalar_eighths // 8
+            cast_columns(nc.scalar.copy, grouped, slabs, 0, split)
+            cast_columns(nc.vector.tensor_copy, grouped, slabs, split, columns)
+            codes = stage.tile([P, columns], U32, name="codes", bufs=3, align_bytes=64)
+            planes = stage.tile([P, columns], U8, name="planes", bufs=3, align_bytes=64)
+            nc.vector.quantize_mx(out=codes[:].bitcast(FP8X4), scales=planes[:], in_=grouped[:])
+            if bank is None:
+                acc = psum.tile([P, width // P, experts * C], F32, name="mm", bufs=2)
+            else:
+                acc = psum.tile([P, width // P, experts * C], F32, name="tied_acc", tag=bank, bufs=1)
+            for q in range(width // P):
+                for i in range(experts):
+                    chunk, u0 = divmod((e0 + i) * C, GATHER_SLOTS)
+                    for s in range(PASSES):
+                        col = (PASSES * i + s) * width + q * P
+                        nc.tensor.matmul_mx(
+                            out=acc[:, q, i * C : (i + 1) * C],
+                            lhsT=codes[:, col : col + P].bitcast(FP8X4),
+                            lhsT_scale=planes[:, col : col + P],
+                            rhs=xg[chunk][s][:, u0 : u0 + C].bitcast(FP8X4),
+                            rhs_scale=xsg[chunk][4 * s : P, u0 : u0 + C],
+                            start=(s == 0),
+                            stop=(s == PASSES - 1),
+                        )
+            for q in range(width // P):
+                nc.scalar.activation(out=h[c0 // P + q][:, e0 * C : (e0 + experts) * C], in_=acc[:, q, :], func=GELU)
+
+        def gather_tokens(c):
+            entries = offs_sb[:, c * GATHER_SLOTS // 16 : (c + 1) * GATHER_SLOTS // 16]
+            xg[c] = [stage.tile([P, GATHER_SLOTS], U32, name="xg", tag="first%d" % (2 * c - 2 + s), bufs=1, align_bytes=64) for s in range(PASSES)]
+            xsg[c] = keep.tile([P, GATHER_SLOTS], U8, name="xsg%d" % c, align_bytes=64)
+            for s in range(PASSES):
+                nc.vector.tensor_copy(xg[c][s][:], xw[:, s, :].bitcast(U32).indirect(entries))
+            nc.vector.tensor_copy(xsg[c][:], xs[:].indirect(entries))
+
+        def load_tokens():
+            nc.sync.dma_start(out=xw[:], in_=x_words.rearrange("s p t d -> p s (t d)").bitcast(I32))
+            nc.sync.dma_start(offs_sb[:], offs)
+
+        def load_token_scales():
+            for quad in range(4):
+                nc.sync.dma_start(
+                    out=xs[32 * quad : 32 * quad + 4 * PASSES, :].bitcast(I32),
+                    in_=x_scales[:, 4 * quad : 4 * quad + 4, :].bitcast(I32),
+                )
+
+        def load_gate():
+            for r in range(2):
+                nc.sync.dma_start(
+                    out=gate_rows[TOKEN_TILES * r : TOKEN_TILES * (r + 1), :],
+                    in_=gate[r, 0, :].rearrange("(j c) -> j c", c=P),
+                )
+
+        def spread_gate():
+            turned = psum.tile([P, 4, P], F32, name="gate_turned", tag="bank0", bufs=1)
+            nc.tensor.transpose(turned[:, 0, :], gate_rows[:], ident[:])
+            nc.scalar.copy(out=gate_cols[:], in_=turned[:, 0, 0:16])
+            for r in range(2):
+                for a in range(0, TOKEN_TILES, 4):
+                    b = min(a + 4, TOKEN_TILES)
+                    spread = psum.tile([P, 4, P], F32, name="spread", tag="bank%d" % (2 * r + a // 4), bufs=1)
+                    for j in range(a, b):
+                        col = TOKEN_TILES * r + j
+                        nc.tensor.transpose(spread[:, j - a, :], gate_cols[:, col : col + 1].to_broadcast([P, P]), ident[:])
+                    nc.scalar.copy(out=gate_sb[r][:, a * P : b * P], in_=spread[:, 0 : b - a, :].rearrange("p j c -> p (j c)"))
+
+        def load_lists():
+            nc.sync.dma_start(pos_sb[0][:], pos1)
+            nc.sync.dma_start(pos_sb[1][:], pos2)
+
+        def load_w2():
+            nc.sync.dma_start(out=w2_raw[:], in_=w2_words[0].rearrange("p n d -> p (n d)").bitcast(I32))
+
+        def load_w2_scales():
+            for quad in range(4):
+                nc.sync.dma_start(
+                    out=s2_raw[32 * quad : 32 * quad + 4, :].bitcast(I32),
+                    in_=w2_scales[0, 4 * quad : 4 * quad + 4, :].bitcast(I32),
+                )
+
+        def deal_w2():
+            nc.vector.tensor_copy(out=w2_codes[:].rearrange("p (t m) -> p t m", t=4), in_=w2_raw[:].rearrange("p (m t) -> p t m", t=4))
+            nc.vector.tensor_copy(out=w2_planes[:].rearrange("p (t m) -> p m t", t=4), in_=s2_raw[:].rearrange("p (m t) -> p m t", t=4))
+
+        def gather_weighted(q, a, b, r, tie):
+            part = stage.tile([P, (b - a) * P], F32, name="part", tag=tie, bufs=1, align_bytes=64)
+            entries = pos_sb[r][:, a * P // 16 : b * P // 16]
+            nc.vector.tensor_tensor(part[:], h[q][:].indirect(entries), gate_sb[r][:, a * P : b * P], MULT)
+            return part
+
+        def turn_and_round(q, groups, parts, bank):
+            first, end = GROUPS[groups[0]][0], GROUPS[groups[-1]][1]
+            turned = psum.tile([P, end - first, P], F32, name="turned", tag=bank, bufs=1)
+            for j in range(end - first):
+                for r in range(2):
+                    nc.tensor.matmul(
+                        turned[:, j, :], lhsT=parts[r][:, j * P : (j + 1) * P], rhs=ident[:],
+                        is_transpose=True, start=(r == 0), stop=(r == 1),
+                    )
+            for g in groups:
+                a, b = GROUPS[g]
+                nc.scalar.copy(
+                    out=c_rows[g][:].rearrange("p j (u w e) -> p j u w e", u=2, e=2)[:, :, :, 32 * q : 32 * (q + 1), :],
+                    in_=turned[:, a - first : b - first, :].rearrange("p j (w u e) -> p j u w e", u=2, e=2),
+                )
+
+        def second_product(g, tie, bank):
+            a, b = GROUPS[g]
+            n = (b - a) * P
+            back = psum.tile([P, 2, 2, P], F32, name="back", tag=bank, bufs=1)
+            words = c_rows[g][:].bitcast(F32)
+            for j in range(b - a):
+                for u in range(2):
+                    nc.tensor.transpose(back[:, j, u, :], words[:, j, u * P : (u + 1) * P], ident[:])
+            c_grouped = stage.tile([P, 4 * n], BF16, name="c_grouped", tag=tie, bufs=1, align_bytes=64)
+            nc.scalar.copy(
+                out=c_grouped[:].bitcast(F32).rearrange("p (j t u) -> p j t u", t=P, u=2),
+                in_=back[:, 0 : b - a, :, :].rearrange("p j u t -> p j t u"),
+            )
+            c_codes = stage.tile([P, n], U32, name="c_codes", align_bytes=64)
+            c_planes = stage.tile([P, n], U8, name="c_planes", align_bytes=64)
+            nc.vector.quantize_mx(out=c_codes[:].bitcast(FP8X4), scales=c_planes[:], in_=c_grouped[:])
+            result = stage.tile([P, 4, n], F32, name="result", bufs=3)
+            for j in range(b - a):
+                acc = psum.tile([P, 4, P], F32, name="mm", bufs=2)
+                for t in range(4):
+                    nc.tensor.matmul_mx(
+                        out=acc[:, t, :],
+                        lhsT=w2_codes[:, t * P : (t + 1) * P].bitcast(FP8X4),
+                        lhsT_scale=w2_planes[:, t * P : (t + 1) * P],
+                        rhs=c_codes[:, j * P : (j + 1) * P].bitcast(FP8X4),
+                        rhs_scale=c_planes[:, j * P : (j + 1) * P],
+                        start=True,
+                        stop=True,
+                    )
+                nc.scalar.copy(out=result[:, :, j * P : (j + 1) * P], in_=acc[:])
+            nc.sync.dma_start(out=out_0.rearrange("(p t) n -> p t n", t=4)[:, :, a * P : b * P], in_=result[:])
+            rounded = stage.tile([P, 4 * n], BF16, name="rounded", align_bytes=64)
+            cast(nc.vector.tensor_copy, rounded, result, 0, n)
+            out_codes = stage.tile([P, n], I32, name="out_codes", bufs=3, align_bytes=64)
+            nc.vector.quantize_mx(out=out_codes[:].bitcast(FP8X4), scales=out_scales[:, a * P : b * P], in_=rounded[:])
+            nc.sync.dma_start(
+                out=out_1[0].rearrange("p t d -> p (t d)").bitcast(I32)[:, a * P : b * P], in_=out_codes[:]
+            )
+
+        extras = {
+            (0, 0, 0): [load_tokens, load_token_scales],
+            (0, 0, 3): [load_gate, spread_gate],
+            (2, 0, 3): [load_lists],
+            (4, 0, 3): [load_w2],
+            (6, 0, 3): [load_w2_scales, deal_w2],
+        }
+        every = list(range(len(GROUPS)))
+
+        for e0 in range(0, E, 2):
+            raw = load_group(e0, e0 + 2, 0, 2 * P)
+            gather_tokens(e0 // 2)
+            for i in range(2):
+                expert_unit(raw[:, PASSES * i : PASSES * (i + 1), :, :], e0 + i, 0, 5, "first%d" % (e0 + i) if e0 + i < E - 2 else None, None)
+
+        def quarter_phase(q, loads, scalar_eighths, earlier, start):
+            unit = 0
+            e0 = 0
+            parts = []
+            for experts in loads:
+                raw = load_group(e0, e0 + experts, q * P, (q + 1) * P)
+                for i in range(0, experts, 2):
+                    n = min(2, experts - i)
+                    k = unit - start
+                    tie = "tie%d_%d" % (q, k) if 0 <= k < 2 * len(earlier) else None
+                    closes = k >= 2 and k % 2 == 0 and k <= 2 * len(earlier)
+                    expert_unit(raw[:, PASSES * i : PASSES * (i + n), :, :], e0 + i, q * P, scalar_eighths, tie, "wide" if closes else None)
+                    if closes:
+                        turn_and_round(earlier[k // 2 - 1], every, parts, "wide")
+                        parts = []
+                    if tie is not None:
+                        parts.append(gather_weighted(earlier[k // 2], 0, TOKEN_TILES, k % 2, tie))
+                    unit = unit + 1
+                e0 = e0 + experts
+
+        quarter_phase(2, (4, 4, 2), 7, [0, 1], 0)
+        quarter_phase(3, (4, 4, 1, 1), 5, [2], 1)
+
+        last = QUARTERS - 1
+
+        def last_parts(g):
+            return [gather_weighted(last, GROUPS[g][0], GROUPS[g][1], r, "end%d_%d" % (g, r)) for r in range(2)]
+
+        turn_and_round(last, [0], last_parts(0), "bank0")
+        parts = last_parts(1)
+        second_product(0, "end2_1", "bank1")
+        turn_and_round(last, [1], parts, "bank1")
+        turn_and_round(last, [2], last_parts(2), "bank2")
+        second_product(1, "c1", "bank3")
+        second_product(2, "c2", "bank0")
+        for quad in range(4):
+            queue = nc.sync if quad % 2 == 0 else nc.scalar
+            queue.dma_start(
+                out=out_2[0, 4 * quad : 4 * quad + 4, :].bitcast(I32),
+                in_=out_scales[32 * quad : 32 * quad + 4, :].bitcast(I32),
+            )

@@ -21,8 +21,9 @@ PASSES = K // 512
 QUARTERS = H // P
 SLOTS = E * C
 TOKEN_TILES = T // P
+WHOLE_EXPERTS = 2
 GATHER_SLOTS = 256
-GROUPS = ((0, 2), (2, 4), (4, 5))
+GROUPS = ((0, 2), (2, 3), (3, 4), (4, 5))
 
 
 def tile_moe_sdn_lin_gelu_kernel(
@@ -42,14 +43,12 @@ def tile_moe_sdn_lin_gelu_kernel(
         ident = keep.tile([P, P], F32, name="ident")
         gate_rows = keep.tile([P, P], F32, name="gate_rows")
         gate_cols = keep.tile([P, 16], F32, name="gate_cols")
-        gate_sb = [keep.tile([P, T], F32, name="gate%d_sb" % r) for r in range(2)]
+        gate_sb = keep.tile([P, 2 * T], F32, name="gate_sb")
         w2_raw = keep.tile([P, N], I32, name="w2_raw")
         s2_raw = keep.tile([P, N], U8, name="s2_raw")
         w2_codes = keep.tile([P, N], I32, name="w2_codes", align_bytes=64)
         w2_planes = keep.tile([P, N], U8, name="w2_planes", align_bytes=64)
         h = [keep.tile([P, SLOTS], F32, name="h%d" % q) for q in range(QUARTERS)]
-        xg = {}
-        xsg = {}
         c_rows = [keep.tile([P, b - a, H], BF16, name="c_rows%d" % a) for a, b in GROUPS]
         out_scales = keep.tile([P, T], U8, name="out_scales", align_bytes=64)
 
@@ -58,18 +57,15 @@ def tile_moe_sdn_lin_gelu_kernel(
         nc.vector.memset(gate_rows[:], 0.0)
         make_identity(nc, ident[:])
 
-        def load_group(e0, e1, c0, c1):
-            slabs = PASSES * (e1 - e0)
-            raw = stage.tile([P, slabs, 4, c1 - c0], F32, name="raw", bufs=5)
-            rows = w1[e0:e1, :, c0:c1].rearrange("e (s p j) c -> p (e s) j c", p=P, j=4)
-            if slabs > 4:
-                for j in range(4):
-                    nc.sync.dma_start(out=raw[:, :, j, :], in_=rows[:, :, j, :])
+        def load_slabs(e, passes, c0, c1, tie):
+            if tie is None:
+                raw = stage.tile([P, len(passes), 4, c1 - c0], F32, name="raw", bufs=8)
             else:
-                for i in range(slabs):
-                    nc.sync.dma_start(out=raw[:, i, :, :], in_=rows[:, i, :, :])
-                    for extra in extras.pop((e0, c0, i), []):
-                        extra()
+                raw = stage.tile([P, len(passes), 4, c1 - c0], F32, name="tied_raw", tag=tie, bufs=1, align_bytes=64)
+            for i, s in enumerate(passes):
+                nc.sync.dma_start(out=raw[:, i, :, :], in_=w1[e, 512 * s : 512 * (s + 1), c0:c1].rearrange("(p j) c -> p j c", j=4))
+                for extra in extras.pop((e, s), []):
+                    extra()
             return raw
 
         def cast(engine_copy, grouped, raw, a, b):
@@ -78,71 +74,52 @@ def tile_moe_sdn_lin_gelu_kernel(
                 in_=raw[:, :, a:b].rearrange("p j (c i) -> p c j i", i=4),
             )
 
-        def cast_columns(engine_copy, grouped, slabs, a, b):
-            width = slabs.shape[3]
-            while a < b:
-                i, c = divmod(a, width)
-                if c == 0 and b - a >= width:
-                    n = (b - a) // width
-                    engine_copy(
-                        out=grouped[:, 4 * a : 4 * (a + n * width)].rearrange("p (s c i j) -> p s c j i", s=n, i=4, j=4),
-                        in_=slabs[:, i : i + n, :, :].rearrange("p s j (c i) -> p s c j i", i=4),
-                    )
-                    a = a + n * width
-                else:
-                    end = min(b, (i + 1) * width)
-                    engine_copy(
-                        out=grouped[:, 4 * a : 4 * end].rearrange("p (c i j) -> p c j i", i=4, j=4),
-                        in_=slabs[:, i, :, c : end - i * width].rearrange("p j (c i) -> p c j i", i=4),
-                    )
-                    a = end
-
-        def expert_unit(slabs, e0, c0, scalar_eighths, tie, bank):
-            count, width = slabs.shape[1], slabs.shape[3]
-            experts = count // PASSES
-            columns = count * width
+        def quantize_slabs(raw, engine_copy, tie):
+            count, width = raw.shape[1], raw.shape[3]
             if tie is None:
-                grouped = stage.tile([P, 4 * columns], BF16, name="grouped", bufs=3, align_bytes=64)
+                grouped = stage.tile([P, 4 * count * width], BF16, name="grouped", bufs=4, align_bytes=64)
             else:
-                grouped = stage.tile([P, 4 * columns], BF16, name="tied_grouped", tag=tie, bufs=1, align_bytes=64)
-            split = columns * scalar_eighths // 8
-            cast_columns(nc.scalar.copy, grouped, slabs, 0, split)
-            cast_columns(nc.vector.tensor_copy, grouped, slabs, split, columns)
-            codes = stage.tile([P, columns], U32, name="codes", bufs=3, align_bytes=64)
-            planes = stage.tile([P, columns], U8, name="planes", bufs=3, align_bytes=64)
+                grouped = stage.tile([P, 4 * count * width], BF16, name="tied_grouped", tag=tie, bufs=1, align_bytes=64)
+            engine_copy(
+                out=grouped[:].rearrange("p (s c i j) -> p s c j i", s=count, i=4, j=4),
+                in_=raw[:].rearrange("p s j (c i) -> p s c j i", i=4),
+            )
+            codes = stage.tile([P, count * width], U32, name="codes", bufs=6, align_bytes=64)
+            planes = stage.tile([P, count * width], U8, name="planes", bufs=6, align_bytes=64)
             nc.vector.quantize_mx(out=codes[:].bitcast(FP8X4), scales=planes[:], in_=grouped[:])
-            if bank is None:
-                acc = psum.tile([P, width // P, experts * C], F32, name="mm", bufs=2)
-            else:
-                acc = psum.tile([P, width // P, experts * C], F32, name="tied_acc", tag=bank, bufs=1)
-            for q in range(width // P):
-                for i in range(experts):
-                    chunk, u0 = divmod((e0 + i) * C, GATHER_SLOTS)
-                    for s in range(PASSES):
-                        col = (PASSES * i + s) * width + q * P
-                        nc.tensor.matmul_mx(
-                            out=acc[:, q, i * C : (i + 1) * C],
-                            lhsT=codes[:, col : col + P].bitcast(FP8X4),
-                            lhsT_scale=planes[:, col : col + P],
-                            rhs=xg[chunk][s][:, u0 : u0 + C].bitcast(FP8X4),
-                            rhs_scale=xsg[chunk][4 * s : P, u0 : u0 + C],
-                            start=(s == 0),
-                            stop=(s == PASSES - 1),
-                        )
-            for q in range(width // P):
-                nc.scalar.activation(out=h[c0 // P + q][:, e0 * C : (e0 + experts) * C], in_=acc[:, q, :], func=GELU)
+            return [(codes[:, i * width : (i + 1) * width], planes[:, i * width : (i + 1) * width]) for i in range(count)]
 
-        def gather_tokens(c):
+        def first_product(e, by_pass, accs, place):
+            chunk, u0 = divmod(e * C, GATHER_SLOTS)
+            for i, acc in enumerate(accs):
+                for s in range(PASSES):
+                    codes, planes = by_pass[s]
+                    nc.tensor.matmul_mx(
+                        out=acc[:, place * C : (place + 1) * C],
+                        lhsT=codes[:, i * P : (i + 1) * P].bitcast(FP8X4),
+                        lhsT_scale=planes[:, i * P : (i + 1) * P],
+                        rhs=gathered[3 * chunk + s][:, u0 : u0 + C].bitcast(FP8X4),
+                        rhs_scale=gathered[3 * chunk + 2][4 * s : P, u0 : u0 + C],
+                        start=(s == 0),
+                        stop=(s == PASSES - 1),
+                    )
+
+        gathered = []
+
+        def gather_tokens(tie):
+            c, sort = divmod(len(gathered), 3)
             entries = offs_sb[:, c * GATHER_SLOTS // 16 : (c + 1) * GATHER_SLOTS // 16]
-            xg[c] = [stage.tile([P, GATHER_SLOTS], U32, name="xg", tag="first%d" % (2 * c - 2 + s), bufs=1, align_bytes=64) for s in range(PASSES)]
-            xsg[c] = keep.tile([P, GATHER_SLOTS], U8, name="xsg%d" % c, align_bytes=64)
-            for s in range(PASSES):
-                nc.vector.tensor_copy(xg[c][s][:], xw[:, s, :].bitcast(U32).indirect(entries))
-            nc.vector.tensor_copy(xsg[c][:], xs[:].indirect(entries))
+            if sort < PASSES:
+                picked = stage.tile([P, GATHER_SLOTS], U32, name="picked_words", tag=tie, bufs=1, align_bytes=64)
+                nc.vector.tensor_copy(picked[:], xw[:, sort, :].bitcast(U32).indirect(entries))
+            else:
+                picked = stage.tile([P, GATHER_SLOTS], U8, name="picked_scales", tag=tie, bufs=1, align_bytes=64)
+                nc.vector.tensor_copy(picked[:], xs[:].indirect(entries))
+            gathered.append(picked)
 
         def load_tokens():
-            nc.sync.dma_start(out=xw[:], in_=x_words.rearrange("s p t d -> p s (t d)").bitcast(I32))
             nc.sync.dma_start(offs_sb[:], offs)
+            nc.sync.dma_start(out=xw[:], in_=x_words.rearrange("s p t d -> p s (t d)").bitcast(I32))
 
         def load_token_scales():
             for quad in range(4):
@@ -152,24 +129,18 @@ def tile_moe_sdn_lin_gelu_kernel(
                 )
 
         def load_gate():
-            for r in range(2):
-                nc.sync.dma_start(
-                    out=gate_rows[TOKEN_TILES * r : TOKEN_TILES * (r + 1), :],
-                    in_=gate[r, 0, :].rearrange("(j c) -> j c", c=P),
-                )
+            nc.sync.dma_start(out=gate_rows[0 : 2 * TOKEN_TILES, :], in_=gate[:, 0, :].rearrange("r (j c) -> r j c", c=P))
 
         def spread_gate():
-            turned = psum.tile([P, 4, P], F32, name="gate_turned", tag="bank0", bufs=1)
+            turned = psum.tile([P, 4, P], F32, name="gate_turned", tag="bank4", bufs=1)
             nc.tensor.transpose(turned[:, 0, :], gate_rows[:], ident[:])
             nc.scalar.copy(out=gate_cols[:], in_=turned[:, 0, 0:16])
-            for r in range(2):
-                for a in range(0, TOKEN_TILES, 4):
-                    b = min(a + 4, TOKEN_TILES)
-                    spread = psum.tile([P, 4, P], F32, name="spread", tag="bank%d" % (2 * r + a // 4), bufs=1)
-                    for j in range(a, b):
-                        col = TOKEN_TILES * r + j
-                        nc.tensor.transpose(spread[:, j - a, :], gate_cols[:, col : col + 1].to_broadcast([P, P]), ident[:])
-                    nc.scalar.copy(out=gate_sb[r][:, a * P : b * P], in_=spread[:, 0 : b - a, :].rearrange("p j c -> p (j c)"))
+            for a in range(0, 2 * TOKEN_TILES, 4):
+                b = min(a + 4, 2 * TOKEN_TILES)
+                spread = psum.tile([P, 4, P], F32, name="spread", tag="bank%d" % (5 + a // 4), bufs=1)
+                for col in range(a, b):
+                    nc.tensor.transpose(spread[:, col - a, :], gate_cols[:, col : col + 1].to_broadcast([P, P]), ident[:])
+                nc.scalar.copy(out=gate_sb[:, a * P : b * P], in_=spread[:, 0 : b - a, :].rearrange("p j c -> p (j c)"))
 
         def load_lists():
             nc.sync.dma_start(pos_sb[0][:], pos1)
@@ -189,29 +160,32 @@ def tile_moe_sdn_lin_gelu_kernel(
             nc.vector.tensor_copy(out=w2_codes[:].rearrange("p (t m) -> p t m", t=4), in_=w2_raw[:].rearrange("p (m t) -> p t m", t=4))
             nc.vector.tensor_copy(out=w2_planes[:].rearrange("p (t m) -> p m t", t=4), in_=s2_raw[:].rearrange("p (m t) -> p m t", t=4))
 
-        def gather_weighted(q, a, b, r, tie):
-            part = stage.tile([P, (b - a) * P], F32, name="part", tag=tie, bufs=1, align_bytes=64)
+        def gather_weighted(part, q, a, b, r):
             entries = pos_sb[r][:, a * P // 16 : b * P // 16]
-            nc.vector.tensor_tensor(part[:], h[q][:].indirect(entries), gate_sb[r][:, a * P : b * P], MULT)
-            return part
+            nc.vector.tensor_tensor(part, h[q][:].indirect(entries), gate_sb[:, r * T + a * P : r * T + b * P], MULT)
 
-        def turn_and_round(q, groups, parts, bank):
-            first, end = GROUPS[groups[0]][0], GROUPS[groups[-1]][1]
-            turned = psum.tile([P, end - first, P], F32, name="turned", tag=bank, bufs=1)
-            for j in range(end - first):
-                for r in range(2):
-                    nc.tensor.matmul(
-                        turned[:, j, :], lhsT=parts[r][:, j * P : (j + 1) * P], rhs=ident[:],
-                        is_transpose=True, start=(r == 0), stop=(r == 1),
-                    )
-            for g in groups:
-                a, b = GROUPS[g]
-                nc.scalar.copy(
-                    out=c_rows[g][:].rearrange("p j (u w e) -> p j u w e", u=2, e=2)[:, :, :, 32 * q : 32 * (q + 1), :],
-                    in_=turned[:, a - first : b - first, :].rearrange("p j (w u e) -> p j u w e", u=2, e=2),
+        def turn(turned, parts, j, column):
+            for r in range(2):
+                nc.tensor.matmul(
+                    turned[:, column : column + P], lhsT=parts[r][:, j * P : (j + 1) * P], rhs=ident[:],
+                    is_transpose=True, start=(r == 0), stop=(r == 1),
                 )
 
-        def second_product(g, tie, bank):
+        def round_combined(g, side, turned):
+            nc.scalar.copy(
+                out=c_rows[g][:].rearrange("p j (u w e) -> p j u w e", u=2, e=2)[:, :, :, 64 * side : 64 * (side + 1), :],
+                in_=turned.rearrange("p (j w u e) -> p j u w e", w=64, u=2, e=2),
+            )
+
+        def turn_and_round(g, parts, bank):
+            a, b = GROUPS[g]
+            turned = psum.tile([P, (b - a) * 2 * P], F32, name="turned", tag=bank, bufs=1)
+            for j in range(b - a):
+                for q in range(2):
+                    turn(turned, parts[2 * q : 2 * q + 2], j, (2 * j + q) * P)
+            round_combined(g, 1, turned[:])
+
+        def quantize_combined(g, tie, bank):
             a, b = GROUPS[g]
             n = (b - a) * P
             back = psum.tile([P, 2, 2, P], F32, name="back", tag=bank, bufs=1)
@@ -224,12 +198,17 @@ def tile_moe_sdn_lin_gelu_kernel(
                 out=c_grouped[:].bitcast(F32).rearrange("p (j t u) -> p j t u", t=P, u=2),
                 in_=back[:, 0 : b - a, :, :].rearrange("p j u t -> p j t u"),
             )
-            c_codes = stage.tile([P, n], U32, name="c_codes", align_bytes=64)
-            c_planes = stage.tile([P, n], U8, name="c_planes", align_bytes=64)
+            c_codes = stage.tile([P, n], U32, name="c_codes", bufs=len(GROUPS), align_bytes=64)
+            c_planes = stage.tile([P, n], U8, name="c_planes", bufs=len(GROUPS), align_bytes=64)
             nc.vector.quantize_mx(out=c_codes[:].bitcast(FP8X4), scales=c_planes[:], in_=c_grouped[:])
-            result = stage.tile([P, 4, n], F32, name="result", bufs=3)
+            return c_codes, c_planes
+
+        def second_product(g, c_codes, c_planes):
+            a, b = GROUPS[g]
+            n = (b - a) * P
+            result = stage.tile([P, 4, n], F32, name="result", bufs=len(GROUPS))
             for j in range(b - a):
-                acc = psum.tile([P, 4, P], F32, name="mm", bufs=2)
+                acc = psum.tile([P, 4, P], F32, name="acc2", tag=("bank3", "bank0", "bank1", "bank2")[(a + j) % 4], bufs=1)
                 for t in range(4):
                     nc.tensor.matmul_mx(
                         out=acc[:, t, :],
@@ -244,62 +223,94 @@ def tile_moe_sdn_lin_gelu_kernel(
             nc.sync.dma_start(out=out_0.rearrange("(p t) n -> p t n", t=4)[:, :, a * P : b * P], in_=result[:])
             rounded = stage.tile([P, 4 * n], BF16, name="rounded", align_bytes=64)
             cast(nc.vector.tensor_copy, rounded, result, 0, n)
-            out_codes = stage.tile([P, n], I32, name="out_codes", bufs=3, align_bytes=64)
+            out_codes = stage.tile([P, n], I32, name="out_codes", bufs=len(GROUPS), align_bytes=64)
             nc.vector.quantize_mx(out=out_codes[:].bitcast(FP8X4), scales=out_scales[:, a * P : b * P], in_=rounded[:])
             nc.sync.dma_start(
                 out=out_1[0].rearrange("p t d -> p (t d)").bitcast(I32)[:, a * P : b * P], in_=out_codes[:]
             )
 
-        extras = {
-            (0, 0, 0): [load_tokens, load_token_scales],
-            (0, 0, 3): [load_gate, spread_gate],
-            (2, 0, 3): [load_lists],
-            (4, 0, 3): [load_w2],
-            (6, 0, 3): [load_w2_scales, deal_w2],
-        }
         every = list(range(len(GROUPS)))
+        token_gathers = 3 * SLOTS // GATHER_SLOTS
+        half = H // 2
+        extras = {
+            (2, 1): [load_lists],
+            (5, 0): [load_w2],
+            (5, 1): [load_w2_scales, deal_w2],
+        }
+        gather_after = [0, 0, 1, 1, 2, 3]
 
-        for e0 in range(0, E, 2):
-            raw = load_group(e0, e0 + 2, 0, 2 * P)
-            gather_tokens(e0 // 2)
-            for i in range(2):
-                expert_unit(raw[:, PASSES * i : PASSES * (i + 1), :, :], e0 + i, 0, 5, "first%d" % (e0 + i) if e0 + i < E - 2 else None, None)
+        on_scalar, on_vector = nc.scalar.copy, nc.vector.tensor_copy
 
-        def quarter_phase(q, loads, scalar_eighths, earlier, start):
-            unit = 0
-            e0 = 0
-            parts = []
-            for experts in loads:
-                raw = load_group(e0, e0 + experts, q * P, (q + 1) * P)
-                for i in range(0, experts, 2):
-                    n = min(2, experts - i)
-                    k = unit - start
-                    tie = "tie%d_%d" % (q, k) if 0 <= k < 2 * len(earlier) else None
-                    closes = k >= 2 and k % 2 == 0 and k <= 2 * len(earlier)
-                    expert_unit(raw[:, PASSES * i : PASSES * (i + n), :, :], e0 + i, q * P, scalar_eighths, tie, "wide" if closes else None)
-                    if closes:
-                        turn_and_round(earlier[k // 2 - 1], every, parts, "wide")
-                        parts = []
-                    if tie is not None:
-                        parts.append(gather_weighted(earlier[k // 2], 0, TOKEN_TILES, k % 2, tie))
-                    unit = unit + 1
-                e0 = e0 + experts
+        warm = keep.tile([P, 1], F32, name="warm")
+        nc.scalar.activation(out=warm[:], in_=ident[:, 0:1], func=GELU)
+        load_gate()
+        load_tokens()
+        load_token_scales()
+        spread_gate()
+        def run_of_experts(e0, e1, q0, q1, first_bank, ties, whole_on_scalar):
+            accs = [psum.tile([P, (e1 - e0) * C], F32, name="acc", tag="bank%d" % (first_bank + q - q0), bufs=1) for q in range(q0, q1)]
+            for e in range(e0, e1):
+                tie, follow = ties.get(e, (None, None))
+                if e in whole_on_scalar:
+                    by_pass = quantize_slabs(load_slabs(e, range(PASSES), q0 * P, q1 * P, tie), on_scalar, None)
+                else:
+                    raws = [load_slabs(e, [s], q0 * P, q1 * P, tie if s == 1 else None) for s in range(PASSES)]
+                    count = gather_after.count(e) if q0 == 0 else 0
+                    picks = ["first%d" % (len(gathered) + i) for i in range(count)] + [None] * (PASSES - count)
+                    by_pass = quantize_slabs(raws[0], on_scalar, picks[0]) + quantize_slabs(raws[1], on_vector, picks[1])
+                    for i in range(count):
+                        gather_tokens(picks[i])
+                first_product(e, by_pass, accs, e - e0)
+                if follow is not None:
+                    whole_part(*follow, tie)
+            for q in range(q0, q1):
+                nc.scalar.activation(out=h[q][:, e0 * C : e1 * C], in_=accs[q - q0][:], func=GELU)
 
-        quarter_phase(2, (4, 4, 2), 7, [0, 1], 0)
-        quarter_phase(3, (4, 4, 1, 1), 5, [2], 1)
+        early = {}
+        early_turned = []
 
-        last = QUARTERS - 1
+        def whole_part(q, r, tie):
+            part = stage.tile([P, T], F32, name="part", tag=tie, bufs=1, align_bytes=64)
+            gather_weighted(part[:], q, 0, TOKEN_TILES, r)
+            early[r] = part
+            if r == 1:
+                if q == 0:
+                    early_turned.extend(psum.tile([P, 4 * P], F32, name="early_turned", tag=bank, bufs=1) for bank in ("bank0", "bank1", "bank2"))
+                for j in range(TOKEN_TILES):
+                    turn(early_turned[j // 2], early, j, (2 * (j % 2) + q) * P)
 
-        def last_parts(g):
-            return [gather_weighted(last, GROUPS[g][0], GROUPS[g][1], r, "end%d_%d" % (g, r)) for r in range(2)]
+        for i in range(token_gathers - len(gather_after)):
+            gather_tokens("first%d" % i)
+        run_of_experts(0, 2, 0, 4, 0, {}, ())
+        run_of_experts(2, 6, 0, 2, 4, {}, ())
+        run_of_experts(6, E, 0, 2, 6, {}, ())
+        whole_part(0, 0, "part0")
+        run_of_experts(2, 6, 2, 4, 3, {3: ("second0", (0, 1)), 5: ("second1", (1, 0))}, (2, 3, 5))
+        run_of_experts(6, E - 1, 2, 4, 5, {}, (7,))
+        run_of_experts(E - 1, E, 2, 3, 7, {}, ())
+        run_of_experts(E - 1, E, 3, 4, 3, {E - 1: ("second2", (1, 1))}, ())
+        for g, (a, b) in enumerate(GROUPS):
+            round_combined(g, 0, early_turned[a // 2][:, (a % 2) * 2 * P : (a % 2 + b - a) * 2 * P])
 
-        turn_and_round(last, [0], last_parts(0), "bank0")
-        parts = last_parts(1)
-        second_product(0, "end2_1", "bank1")
-        turn_and_round(last, [1], parts, "bank1")
-        turn_and_round(last, [2], last_parts(2), "bank2")
-        second_product(1, "c1", "bank3")
-        second_product(2, "c2", "bank0")
+        def last_parts(g, tie):
+            a, b = GROUPS[g]
+            four = stage.tile([P, 4, (b - a) * P], F32, name="four", tag=tie, bufs=1, align_bytes=64)
+            for i in range(4):
+                gather_weighted(four[:, i, :], 2 + i // 2, a, b, i % 2)
+            return [four[:, i, :] for i in range(4)]
+
+        turn_and_round(0, last_parts(0, "end0"), "bank4")
+        turn_and_round(1, last_parts(1, "end1"), "bank5")
+        parts = last_parts(2, "end2")
+        combined = [quantize_combined(0, "end3", "bank6")]
+        turn_and_round(2, parts, "bank6")
+        combined.append(quantize_combined(1, "c1", "bank7"))
+        turn_and_round(3, last_parts(3, "end3"), "bank4")
+        combined.append(quantize_combined(2, "c2", "bank5"))
+        second_product(0, *combined[0])
+        combined.append(quantize_combined(3, "c3", "bank7"))
+        for g in range(1, len(GROUPS)):
+            second_product(g, *combined[g])
         for quad in range(4):
             queue = nc.sync if quad % 2 == 0 else nc.scalar
             queue.dma_start(

from contextlib import ExitStack

import concourse.mybir as mybir
from concourse.masks import make_identity

K, T, E, C, H, N = 1024, 640, 10, 128, 512, 512
FLOPS = 2 * E * C * K * H + 2 * T * H * N

F32 = mybir.dt.float32
BF16 = mybir.dt.bfloat16
I32 = mybir.dt.int32
U32 = mybir.dt.uint32
U16 = mybir.dt.uint16
U8 = mybir.dt.uint8
FP8X4 = mybir.dt.float8_e4m3fn_x4
MULT = mybir.AluOpType.mult
GELU = mybir.ActivationFunctionType.Gelu_apprx_tanh

P = 128
PASSES = K // 512
QUARTERS = H // P
SLOTS = E * C
TOKEN_TILES = T // P
WHOLE_EXPERTS = 2
GATHER_SLOTS = 256
GROUPS = ((0, 2), (2, 3), (3, 4), (4, 5))


def tile_moe_sdn_lin_gelu_kernel(
    tc, x_words, x_scales, w1, w2_words, w2_scales, gate, offs, pos1, pos2, out_0, out_1, out_2
):
    nc = tc.nc
    with ExitStack() as ctx:
        lists = ctx.enter_context(tc.tile_pool(name="lists", bufs=1))
        keep = ctx.enter_context(tc.tile_pool(name="keep", bufs=1))
        stage = ctx.enter_context(tc.tile_pool(name="stage", bufs=2))
        psum = ctx.enter_context(tc.psum_pool(name="psum", bufs=1))

        offs_sb = lists.tile([P, SLOTS // 16], U16, name="offs_sb")
        pos_sb = [lists.tile([P, T // 16], U16, name="pos%d_sb" % r) for r in range(2)]
        xw = keep.tile([P, PASSES, T], I32, name="xw", align_bytes=64)
        xs = keep.tile([P, T], U8, name="xs", align_bytes=64)
        ident = keep.tile([P, P], F32, name="ident")
        gate_rows = keep.tile([P, P], F32, name="gate_rows")
        gate_cols = keep.tile([P, 16], F32, name="gate_cols")
        gate_sb = keep.tile([P, 2 * T], F32, name="gate_sb")
        w2_raw = keep.tile([P, N], I32, name="w2_raw")
        s2_raw = keep.tile([P, N], U8, name="s2_raw")
        w2_codes = keep.tile([P, N], I32, name="w2_codes", align_bytes=64)
        w2_planes = keep.tile([P, N], U8, name="w2_planes", align_bytes=64)
        h = [keep.tile([P, SLOTS], F32, name="h%d" % q) for q in range(QUARTERS)]
        c_rows = [keep.tile([P, b - a, H], BF16, name="c_rows%d" % a) for a, b in GROUPS]
        out_scales = keep.tile([P, T], U8, name="out_scales", align_bytes=64)

        nc.vector.memset(xs[:].bitcast(I32), 0)
        nc.vector.memset(s2_raw[:].bitcast(I32), 0)
        nc.vector.memset(gate_rows[:], 0.0)
        make_identity(nc, ident[:])

        def load_slabs(e, passes, c0, c1, tie):
            if tie is None:
                raw = stage.tile([P, len(passes), 4, c1 - c0], F32, name="raw", bufs=8)
            else:
                raw = stage.tile([P, len(passes), 4, c1 - c0], F32, name="tied_raw", tag=tie, bufs=1, align_bytes=64)
            for i, s in enumerate(passes):
                nc.sync.dma_start(out=raw[:, i, :, :], in_=w1[e, 512 * s : 512 * (s + 1), c0:c1].rearrange("(p j) c -> p j c", j=4))
                for extra in extras.pop((e, s), []):
                    extra()
            return raw

        def cast(engine_copy, grouped, raw, a, b):
            engine_copy(
                out=grouped[:, 4 * a : 4 * b].rearrange("p (c i j) -> p c j i", i=4, j=4),
                in_=raw[:, :, a:b].rearrange("p j (c i) -> p c j i", i=4),
            )

        def quantize_slabs(raw, engine_copy, tie):
            count, width = raw.shape[1], raw.shape[3]
            if tie is None:
                grouped = stage.tile([P, 4 * count * width], BF16, name="grouped", bufs=4, align_bytes=64)
            else:
                grouped = stage.tile([P, 4 * count * width], BF16, name="tied_grouped", tag=tie, bufs=1, align_bytes=64)
            engine_copy(
                out=grouped[:].rearrange("p (s c i j) -> p s c j i", s=count, i=4, j=4),
                in_=raw[:].rearrange("p s j (c i) -> p s c j i", i=4),
            )
            codes = stage.tile([P, count * width], U32, name="codes", bufs=6, align_bytes=64)
            planes = stage.tile([P, count * width], U8, name="planes", bufs=6, align_bytes=64)
            nc.vector.quantize_mx(out=codes[:].bitcast(FP8X4), scales=planes[:], in_=grouped[:])
            return [(codes[:, i * width : (i + 1) * width], planes[:, i * width : (i + 1) * width]) for i in range(count)]

        def first_product(e, by_pass, accs, place):
            chunk, u0 = divmod(e * C, GATHER_SLOTS)
            for i, acc in enumerate(accs):
                for s in range(PASSES):
                    codes, planes = by_pass[s]
                    nc.tensor.matmul_mx(
                        out=acc[:, place * C : (place + 1) * C],
                        lhsT=codes[:, i * P : (i + 1) * P].bitcast(FP8X4),
                        lhsT_scale=planes[:, i * P : (i + 1) * P],
                        rhs=gathered[3 * chunk + s][:, u0 : u0 + C].bitcast(FP8X4),
                        rhs_scale=gathered[3 * chunk + 2][4 * s : P, u0 : u0 + C],
                        start=(s == 0),
                        stop=(s == PASSES - 1),
                    )

        gathered = []

        def gather_tokens(tie):
            c, sort = divmod(len(gathered), 3)
            entries = offs_sb[:, c * GATHER_SLOTS // 16 : (c + 1) * GATHER_SLOTS // 16]
            if sort < PASSES:
                picked = stage.tile([P, GATHER_SLOTS], U32, name="picked_words", tag=tie, bufs=1, align_bytes=64)
                nc.vector.tensor_copy(picked[:], xw[:, sort, :].bitcast(U32).indirect(entries))
            else:
                picked = stage.tile([P, GATHER_SLOTS], U8, name="picked_scales", tag=tie, bufs=1, align_bytes=64)
                nc.vector.tensor_copy(picked[:], xs[:].indirect(entries))
            gathered.append(picked)

        def load_tokens():
            nc.sync.dma_start(offs_sb[:], offs)
            nc.sync.dma_start(out=xw[:], in_=x_words.rearrange("s p t d -> p s (t d)").bitcast(I32))

        def load_token_scales():
            for quad in range(4):
                nc.sync.dma_start(
                    out=xs[32 * quad : 32 * quad + 4 * PASSES, :].bitcast(I32),
                    in_=x_scales[:, 4 * quad : 4 * quad + 4, :].bitcast(I32),
                )

        def load_gate():
            nc.sync.dma_start(out=gate_rows[0 : 2 * TOKEN_TILES, :], in_=gate[:, 0, :].rearrange("r (j c) -> r j c", c=P))

        def spread_gate():
            turned = psum.tile([P, 4, P], F32, name="gate_turned", tag="bank4", bufs=1)
            nc.tensor.transpose(turned[:, 0, :], gate_rows[:], ident[:])
            nc.scalar.copy(out=gate_cols[:], in_=turned[:, 0, 0:16])
            for a in range(0, 2 * TOKEN_TILES, 4):
                b = min(a + 4, 2 * TOKEN_TILES)
                spread = psum.tile([P, 4, P], F32, name="spread", tag="bank%d" % (5 + a // 4), bufs=1)
                for col in range(a, b):
                    nc.tensor.transpose(spread[:, col - a, :], gate_cols[:, col : col + 1].to_broadcast([P, P]), ident[:])
                nc.scalar.copy(out=gate_sb[:, a * P : b * P], in_=spread[:, 0 : b - a, :].rearrange("p j c -> p (j c)"))

        def load_lists():
            nc.sync.dma_start(pos_sb[0][:], pos1)
            nc.sync.dma_start(pos_sb[1][:], pos2)

        def load_w2():
            nc.sync.dma_start(out=w2_raw[:], in_=w2_words[0].rearrange("p n d -> p (n d)").bitcast(I32))

        def load_w2_scales():
            for quad in range(4):
                nc.sync.dma_start(
                    out=s2_raw[32 * quad : 32 * quad + 4, :].bitcast(I32),
                    in_=w2_scales[0, 4 * quad : 4 * quad + 4, :].bitcast(I32),
                )

        def deal_w2():
            nc.vector.tensor_copy(out=w2_codes[:].rearrange("p (t m) -> p t m", t=4), in_=w2_raw[:].rearrange("p (m t) -> p t m", t=4))
            nc.vector.tensor_copy(out=w2_planes[:].rearrange("p (t m) -> p m t", t=4), in_=s2_raw[:].rearrange("p (m t) -> p m t", t=4))

        def gather_weighted(part, q, a, b, r):
            entries = pos_sb[r][:, a * P // 16 : b * P // 16]
            nc.vector.tensor_tensor(part, h[q][:].indirect(entries), gate_sb[:, r * T + a * P : r * T + b * P], MULT)

        def turn(turned, parts, j, column):
            for r in range(2):
                nc.tensor.matmul(
                    turned[:, column : column + P], lhsT=parts[r][:, j * P : (j + 1) * P], rhs=ident[:],
                    is_transpose=True, start=(r == 0), stop=(r == 1),
                )

        def round_combined(g, side, turned):
            nc.scalar.copy(
                out=c_rows[g][:].rearrange("p j (u w e) -> p j u w e", u=2, e=2)[:, :, :, 64 * side : 64 * (side + 1), :],
                in_=turned.rearrange("p (j w u e) -> p j u w e", w=64, u=2, e=2),
            )

        def turn_and_round(g, parts, bank):
            a, b = GROUPS[g]
            turned = psum.tile([P, (b - a) * 2 * P], F32, name="turned", tag=bank, bufs=1)
            for j in range(b - a):
                for q in range(2):
                    turn(turned, parts[2 * q : 2 * q + 2], j, (2 * j + q) * P)
            round_combined(g, 1, turned[:])

        def quantize_combined(g, tie, bank):
            a, b = GROUPS[g]
            n = (b - a) * P
            back = psum.tile([P, 2, 2, P], F32, name="back", tag=bank, bufs=1)
            words = c_rows[g][:].bitcast(F32)
            for j in range(b - a):
                for u in range(2):
                    nc.tensor.transpose(back[:, j, u, :], words[:, j, u * P : (u + 1) * P], ident[:])
            c_grouped = stage.tile([P, 4 * n], BF16, name="c_grouped", tag=tie, bufs=1, align_bytes=64)
            nc.scalar.copy(
                out=c_grouped[:].bitcast(F32).rearrange("p (j t u) -> p j t u", t=P, u=2),
                in_=back[:, 0 : b - a, :, :].rearrange("p j u t -> p j t u"),
            )
            c_codes = stage.tile([P, n], U32, name="c_codes", bufs=len(GROUPS), align_bytes=64)
            c_planes = stage.tile([P, n], U8, name="c_planes", bufs=len(GROUPS), align_bytes=64)
            nc.vector.quantize_mx(out=c_codes[:].bitcast(FP8X4), scales=c_planes[:], in_=c_grouped[:])
            return c_codes, c_planes

        def second_product(g, c_codes, c_planes):
            a, b = GROUPS[g]
            n = (b - a) * P
            result = stage.tile([P, 4, n], F32, name="result", bufs=len(GROUPS))
            for j in range(b - a):
                acc = psum.tile([P, 4, P], F32, name="acc2", tag=("bank3", "bank0", "bank1", "bank2")[(a + j) % 4], bufs=1)
                for t in range(4):
                    nc.tensor.matmul_mx(
                        out=acc[:, t, :],
                        lhsT=w2_codes[:, t * P : (t + 1) * P].bitcast(FP8X4),
                        lhsT_scale=w2_planes[:, t * P : (t + 1) * P],
                        rhs=c_codes[:, j * P : (j + 1) * P].bitcast(FP8X4),
                        rhs_scale=c_planes[:, j * P : (j + 1) * P],
                        start=True,
                        stop=True,
                    )
                nc.scalar.copy(out=result[:, :, j * P : (j + 1) * P], in_=acc[:])
            nc.sync.dma_start(out=out_0.rearrange("(p t) n -> p t n", t=4)[:, :, a * P : b * P], in_=result[:])
            rounded = stage.tile([P, 4 * n], BF16, name="rounded", align_bytes=64)
            cast(nc.vector.tensor_copy, rounded, result, 0, n)
            out_codes = stage.tile([P, n], I32, name="out_codes", bufs=len(GROUPS), align_bytes=64)
            nc.vector.quantize_mx(out=out_codes[:].bitcast(FP8X4), scales=out_scales[:, a * P : b * P], in_=rounded[:])
            nc.sync.dma_start(
                out=out_1[0].rearrange("p t d -> p (t d)").bitcast(I32)[:, a * P : b * P], in_=out_codes[:]
            )

        every = list(range(len(GROUPS)))
        token_gathers = 3 * SLOTS // GATHER_SLOTS
        half = H // 2
        extras = {
            (2, 1): [load_lists],
            (5, 0): [load_w2],
            (5, 1): [load_w2_scales, deal_w2],
        }
        gather_after = [0, 0, 1, 1, 2, 3]

        on_scalar, on_vector = nc.scalar.copy, nc.vector.tensor_copy

        warm = keep.tile([P, 1], F32, name="warm")
        nc.scalar.activation(out=warm[:], in_=ident[:, 0:1], func=GELU)
        load_gate()
        load_tokens()
        load_token_scales()
        spread_gate()
        def run_of_experts(e0, e1, q0, q1, first_bank, ties, whole_on_scalar):
            accs = [psum.tile([P, (e1 - e0) * C], F32, name="acc", tag="bank%d" % (first_bank + q - q0), bufs=1) for q in range(q0, q1)]
            for e in range(e0, e1):
                tie, follow = ties.get(e, (None, None))
                if e in whole_on_scalar:
                    by_pass = quantize_slabs(load_slabs(e, range(PASSES), q0 * P, q1 * P, tie), on_scalar, None)
                else:
                    raws = [load_slabs(e, [s], q0 * P, q1 * P, tie if s == 1 else None) for s in range(PASSES)]
                    count = gather_after.count(e) if q0 == 0 else 0
                    picks = ["first%d" % (len(gathered) + i) for i in range(count)] + [None] * (PASSES - count)
                    by_pass = quantize_slabs(raws[0], on_scalar, picks[0]) + quantize_slabs(raws[1], on_vector, picks[1])
                    for i in range(count):
                        gather_tokens(picks[i])
                first_product(e, by_pass, accs, e - e0)
                if follow is not None:
                    whole_part(*follow, tie)
            for q in range(q0, q1):
                nc.scalar.activation(out=h[q][:, e0 * C : e1 * C], in_=accs[q - q0][:], func=GELU)

        early = {}
        early_turned = []

        def whole_part(q, r, tie):
            part = stage.tile([P, T], F32, name="part", tag=tie, bufs=1, align_bytes=64)
            gather_weighted(part[:], q, 0, TOKEN_TILES, r)
            early[r] = part
            if r == 1:
                if q == 0:
                    early_turned.extend(psum.tile([P, 4 * P], F32, name="early_turned", tag=bank, bufs=1) for bank in ("bank0", "bank1", "bank2"))
                for j in range(TOKEN_TILES):
                    turn(early_turned[j // 2], early, j, (2 * (j % 2) + q) * P)

        for i in range(token_gathers - len(gather_after)):
            gather_tokens("first%d" % i)
        run_of_experts(0, 2, 0, 4, 0, {}, ())
        run_of_experts(2, 6, 0, 2, 4, {}, ())
        run_of_experts(6, E, 0, 2, 6, {}, ())
        whole_part(0, 0, "part0")
        run_of_experts(2, 6, 2, 4, 3, {3: ("second0", (0, 1)), 5: ("second1", (1, 0))}, (2, 3, 5))
        run_of_experts(6, E - 1, 2, 4, 5, {}, (7,))
        run_of_experts(E - 1, E, 2, 3, 7, {}, ())
        run_of_experts(E - 1, E, 3, 4, 3, {E - 1: ("second2", (1, 1))}, ())
        for g, (a, b) in enumerate(GROUPS):
            round_combined(g, 0, early_turned[a // 2][:, (a % 2) * 2 * P : (a % 2 + b - a) * 2 * P])

        def last_parts(g, tie):
            a, b = GROUPS[g]
            four = stage.tile([P, 4, (b - a) * P], F32, name="four", tag=tie, bufs=1, align_bytes=64)
            for i in range(4):
                gather_weighted(four[:, i, :], 2 + i // 2, a, b, i % 2)
            return [four[:, i, :] for i in range(4)]

        turn_and_round(0, last_parts(0, "end0"), "bank4")
        turn_and_round(1, last_parts(1, "end1"), "bank5")
        parts = last_parts(2, "end2")
        combined = [quantize_combined(0, "end3", "bank6")]
        turn_and_round(2, parts, "bank6")
        combined.append(quantize_combined(1, "c1", "bank7"))
        turn_and_round(3, last_parts(3, "end3"), "bank4")
        combined.append(quantize_combined(2, "c2", "bank5"))
        second_product(0, *combined[0])
        combined.append(quantize_combined(3, "c3", "bank7"))
        for g in range(1, len(GROUPS)):
            second_product(g, *combined[g])
        for quad in range(4):
            queue = nc.sync if quad % 2 == 0 else nc.scalar
            queue.dma_start(
                out=out_2[0, 4 * quad : 4 * quad + 4, :].bitcast(I32),
                in_=out_scales[32 * quad : 32 * quad + 4, :].bitcast(I32),
            )
